import numpy as np
import ml_dtypes


def mxq(x, axis, fmt="e4m3"):
    dtype, down = {"e4m3": (ml_dtypes.float8_e4m3fn, 7), "e5m2": (ml_dtypes.float8_e5m2, 14)}[fmt]
    v = np.moveaxis(np.asarray(x, np.float32).astype(ml_dtypes.bfloat16).astype(np.float64), axis, -1)
    blocks = v.reshape(v.shape[:-1] + (-1, 32))
    amax = np.abs(blocks).max(-1, keepdims=True)
    byte = np.maximum(np.where(amax > 0, np.frexp(amax)[1] - 1 + 127, 0) - down, 1)
    scale = np.exp2(byte - 127.0)
    codes = (blocks / scale).astype(np.float32).astype(dtype).astype(np.float64)
    return np.moveaxis((codes * scale).reshape(v.shape), -1, axis)


WIDE = False


def mx_kscale(k):
    if not WIDE:
        return np.ones(k)
    levels = np.array([10, -10, 5, -5, 0])
    if k % 512:
        return np.exp2(np.random.permutation(np.resize(levels, k // 32))).repeat(32)
    a = np.empty((k // 512, 16))
    for p in range(k // 512):
        a[p, :8] = np.random.permutation(np.resize(levels, 8))
        for g in range(8):
            far = levels[np.abs(levels - a[p, g]) >= 10]
            a[p, g + 8] = far[np.random.randint(len(far))]
    return np.exp2(a.ravel()).repeat(32)


BF16 = ml_dtypes.bfloat16


def bf(x):
    return np.asarray(x, np.float32).astype(BF16)


def f64(x):
    return np.asarray(x).astype(np.float64)


R, A, O = 512, 4, 1024


def setup_inputs():
    s, u = mx_kscale(O), mx_kscale(R)
    return {"x": bf(np.random.standard_normal((R, A, O)) * s * u[:, None, None]),
            "switch_a": bf(np.random.standard_normal((O, O)) / (3 * np.sqrt(O)) / s[:, None] * s),
            "commute": bf(np.random.standard_normal((R, R)) / (3 * np.sqrt(R)) / u * u[:, None]),
            "switch_b": bf(np.random.standard_normal((O, O)) / np.sqrt(O) / s[:, None]),
            "age_gate": bf(np.random.uniform(0.3, 1.0, (A, O))),
            "region_rate": bf((1 + 0.1 * np.random.standard_normal(R)) / u)}


def reference(x, switch_a, commute, switch_b, age_gate, region_rate):
    x = f64(x).reshape(R * A, O)
    d1 = mxq(x, 1, "e4m3") @ mxq(f64(switch_a), 0, "e4m3")
    h1 = (x + d1).reshape(R, A * O)
    d2 = mxq(f64(commute), 1, "e4m3") @ mxq(h1, 0, "e4m3")
    h2 = (h1 + d2).reshape(R * A, O)
    d3 = (mxq(h2, 1, "e4m3") @ mxq(f64(switch_b), 0, "e4m3")).reshape(R, A, O)
    return d3 * f64(age_gate) * f64(region_rate)[:, None, None]

@@ -1,0 +1,309 @@
+from contextlib import ExitStack
+
+import concourse.mybir as mybir
+from concourse.masks import make_identity
+
+R, A, O = 512, 4, 1024
+FLOPS = 2 * R * A * O * O * 2 + 2 * R * R * A * O
+
+F32 = mybir.dt.float32
+BF16 = mybir.dt.bfloat16
+U32 = mybir.dt.uint32
+U8 = mybir.dt.uint8
+FP8X4 = mybir.dt.float8_e4m3fn_x4
+ADD = mybir.AluOpType.add
+MULT = mybir.AluOpType.mult
+COPY = mybir.ActivationFunctionType.Copy
+
+P = 128
+T = 4
+N = 512
+G = O // 512
+
+
+def tile_age_gated_labour_flows_t1_kernel(tc, x, switch_a, commute, switch_b, age_gate, region_rate, out):
+    nc = tc.nc
+    x_v = x.rearrange("(p t) a o -> p t a o", t=T)
+    out_v = out.rearrange("(p t) a o -> p t a o", t=T)
+
+    with ExitStack() as ctx:
+        keep = ctx.enter_context(tc.tile_pool(name="keep", bufs=1))
+        work = ctx.enter_context(tc.tile_pool(name="work", bufs=2))
+        psum = ctx.enter_context(tc.psum_pool(name="psum", bufs=1))
+        ctx.enter_context(tc.manual_schedule())
+
+        x_sb, raw_w, codes_w = {}, {}, {}
+
+        def load_x(a, pieces, i):
+            if i == 0:
+                x_sb[a] = keep.tile([P, T, O], BF16, name=f"x{a}")
+            ts = slice(i * T // pieces, (i + 1) * T // pieces)
+            nc.sync.dma_start(out=x_sb[a][:, ts, :], in_=x_v[:, ts, a, :])
+
+        def load_w(w, which, k, h):
+            t = keep.tile([P, 4, N], BF16, name=f"raw_{which}{k}{h}")
+            nc.sync.dma_start(
+                out=t[:],
+                in_=w[k * 512 : (k + 1) * 512, h * N : (h + 1) * N].rearrange("(p j) o -> p j o", j=4),
+            )
+            raw_w[which, k, h] = t
+
+        ident = keep.tile([P, P], F32, name="ident")
+        make_identity(nc, ident[:])
+
+        load_w(switch_a, "a", 0, 0)
+        load_x(0, 2, 0)
+        load_w(switch_a, "a", 1, 0)
+        load_x(0, 2, 1)
+        load_w(switch_a, "a", 0, 1)
+        load_w(switch_a, "a", 1, 1)
+        c_sb = keep.tile([P, T, R], BF16, name="c_sb")
+        nc.sync.dma_start(out=c_sb[:], in_=commute.rearrange("(p t) i -> p t i", t=T))
+        load_x(1, 1, 0)
+        for h in range(2):
+            for k in range(G):
+                load_w(switch_b, "b", k, h)
+        load_x(2, 1, 0)
+        rate_bf = keep.tile([P, T], BF16, name="rate_bf")
+        nc.sync.dma_start(out=rate_bf[:], in_=region_rate.rearrange("(p t) -> p t", t=T))
+        gate = keep.tile([P, A, O], BF16, name="gate")
+        nc.sync.dma_start(out=gate[:], in_=age_gate.partition_broadcast(P))
+        load_x(3, 1, 0)
+        rate = keep.tile([P, T], F32, name="rate")
+
+        mid_w = {}
+
+        def copy_on(eng, out, in_):
+            if eng == "V":
+                nc.vector.tensor_copy(out=out, in_=in_)
+            elif eng == "S":
+                nc.scalar.copy(out=out, in_=in_)
+            else:
+                nc.gpsimd.tensor_scalar(out=out, in0=in_, scalar1=1.0, scalar2=0.0, op0=MULT, op1=ADD)
+
+        def mid(which, k, h):
+            if (which, k, h) not in mid_w:
+                mid_w[which, k, h] = work.tile([P, N, 4], BF16, name="mid_w", tag="mid_w", bufs=3, align_bytes=64)
+            return mid_w[which, k, h]
+
+        def interleave_a(eng, k, h, u, lo=0, hi=128):
+            raw = raw_w["a", k, h][:].rearrange("p j (q u e) -> p u q e j", u=2, e=2)[:, u, lo:hi]
+            dst = mid("a", k, h)[:].rearrange("p (u q e) j -> p u q e j", u=2, e=2)[:, u, lo:hi]
+            copy_on(eng, dst, raw)
+
+        def interleave_b(eng, k, h, half):
+            cols = slice(half * 256, half * 256 + 256)
+            copy_on(eng, mid("b", k, h)[:, cols, :], raw_w["b", k, h][:, :, cols].rearrange("p j n -> p n j"))
+
+        def quantize(pool, name, bufs, src, width):
+            c = pool.tile([P, width], U32, name=name + "_c", tag=name + "_c", bufs=bufs, align_bytes=64)
+            s = pool.tile([P, width], U8, name=name + "_s", tag=name + "_s", bufs=bufs, align_bytes=64)
+            nc.vector.quantize_mx(out=c[:].bitcast(FP8X4), scales=s[:], in_=src)
+            return c, s
+
+        def quantize_w(which, k, h):
+            codes_w[which, k, h] = quantize(
+                keep, f"w{which}{k}{h}", 1, mid(which, k, h)[:].rearrange("p n j -> p (n j)"), N
+            )
+
+        def mm(acc, lhs, lcols, rhs, k, first, last):
+            nc.tensor.matmul_mx(
+                out=acc[:],
+                lhsT=lhs[0][:, lcols].bitcast(FP8X4),
+                lhsT_scale=lhs[1][:, lcols],
+                rhs=rhs[0][:].bitcast(FP8X4),
+                rhs_scale=rhs[1][:],
+                start=first,
+                stop=last,
+            )
+
+        def acc_tile():
+            return psum.tile([P, N], F32, name="acc", tag="acc", bufs=ACC)
+
+        def turn(words, eng, dst):
+            tr = psum.tile([P, 2, 2, P], F32, name="tr", tag="tr", bufs=8 - ACC)
+            for i in range(2):
+                for u in range(2):
+                    nc.tensor.transpose(tr[:, i, u, :], words(i, u), ident[:])
+            copy_on(eng, dst.bitcast(F32), tr[:].rearrange("p i u r -> p i r u"))
+
+        x_mid, x_codes = {}, {}
+
+        def turn_x(a, t, eng):
+            if t % 2 == 0:
+                x_mid[a, t // 2] = work.tile([P, 2, G, P, 4], BF16, name="x_mid", bufs=2, align_bytes=64)
+            w = x_sb[a][:, t, :].bitcast(F32)
+            turn(lambda k, u: w[:, 256 * k + u : 256 * (k + 1) : 2], eng, x_mid[a, t // 2][:, t % 2])
+
+        def quantize_x(a, pair):
+            x_codes[a, pair] = quantize(work, "x", 4, x_mid[a, pair][:].rearrange("p t k r j -> p (t k r j)"), 4 * P)
+
+        c_codes = []
+
+        def turn_c(eng):
+            w = c_sb[:].bitcast(F32)
+            m = keep.tile([P, T, P, 4], BF16, name="c_mid", align_bytes=64)
+            for pair in range(2):
+                turn(lambda i, u: w[:, 2 * pair + i, u::2], eng, m[:, 2 * pair : 2 * pair + 2])
+            return m
+
+        h1, h1_mid, h1_codes, h2 = {}, {}, {}, {}
+        acc1, acc2, acc3 = {}, {}, {}
+
+        def stage1_mm(a, h, t):
+            acc1[a, h, t] = acc = acc_tile()
+            for k in range(G):
+                mm(acc, x_codes[a, t // 2], slice(((t % 2) * G + k) * P, ((t % 2) * G + k + 1) * P), codes_w["a", k, h], k, k == 0, k == G - 1)
+
+        def stage1_add(a, h, t):
+            if t == 0:
+                h1[a, h] = work.tile([P, T, N], F32, name="h1", bufs=3)
+            nc.vector.tensor_tensor(
+                out=h1[a, h][:, t, :].rearrange("p (u q e) -> p u q e", u=2, e=2),
+                in0=acc1[a, h, t][:].rearrange("p (u q e) -> p u q e", u=2, e=2),
+                in1=x_sb[a][:, t, h * N : (h + 1) * N].rearrange("p (q u e) -> p u q e", u=2, e=2),
+                op=ADD,
+            )
+
+        def cast_h1(a, h, half, eng):
+            if half == 0:
+                h1_mid[a, h] = work.tile([P, N, T], BF16, name="h1_mid", bufs=2, align_bytes=64)
+            cols = slice(half * 256, half * 256 + 256)
+            copy_on(eng, h1_mid[a, h][:, cols, :], h1[a, h][:, :, cols].rearrange("p t n -> p n t"))
+
+        def quantize_h1(a, h):
+            h1_codes[a, h] = quantize(work, "h1q", 2, h1_mid[a, h][:].rearrange("p n t -> p (n t)"), N)
+
+        def stage2_mm(a, h, t):
+            acc2[a, h, t] = acc = acc_tile()
+            mm(acc, c_codes[0], slice(t * P, (t + 1) * P), h1_codes[a, h], 0, True, True)
+
+        def stage2_add(a, h, t):
+            if h == 0:
+                h2[a, t] = work.tile([P, O], BF16, name="h2", bufs=8)
+            nc.vector.tensor_tensor(
+                out=h2[a, t][:, h * N : (h + 1) * N], in0=acc2[a, h, t][:], in1=h1[a, h][:, t, :], op=ADD
+            )
+
+        h2_mid, h2_codes, o_sb = {}, {}, {}
+
+        def turn_h2(a, t, eng):
+            if t % 2 == 0:
+                h2_mid[a, t // 2] = work.tile([P, 2, G, P, 4], BF16, name="h2_mid", bufs=2, align_bytes=64)
+            w = h2[a, t][:].bitcast(F32)
+            turn(lambda k, u: w[:, (2 * k + u) * P : (2 * k + u + 1) * P], eng, h2_mid[a, t // 2][:, t % 2])
+
+        def quantize_h2(a, pair):
+            h2_codes[a, pair] = quantize(work, "h2q", 4, h2_mid[a, pair][:].rearrange("p t k r j -> p (t k r j)"), 4 * P)
+
+        def stage3_mm(a, t, h):
+            acc3[a, t, h] = acc = acc_tile()
+            for k in range(G):
+                mm(acc, h2_codes[a, t // 2], slice(((t % 2) * G + k) * P, ((t % 2) * G + k + 1) * P), codes_w["b", k, h], k, k == 0, k == G - 1)
+
+        def stage3_out(a, t, h, eng):
+            if h == 0:
+                o_sb[a, t] = work.tile([P, O], F32, name="o_sb", bufs=5)
+            acc = acc3[a, t, h]
+            o = o_sb[a, t][:, h * N : (h + 1) * N]
+            g = gate[:, a, h * N : (h + 1) * N]
+            if eng == "V":
+                nc.vector.scalar_tensor_tensor(out=o, in0=acc[:], scalar=rate[:, t : t + 1], in1=g, op0=MULT, op1=MULT)
+            else:
+                tmp = work.tile([P, N], F32, name="tmp", bufs=2)
+                nc.scalar.activation(out=tmp[:], in_=acc[:], func=COPY, scale=rate[:, t : t + 1])
+                nc.gpsimd.tensor_tensor(out=o, in0=tmp[:], in1=g, op=MULT)
+            if a == A - 1:
+                nc.sync.dma_start(out=out_v[:, t, a, h * N : (h + 1) * N], in_=o)
+            elif h == 1:
+                nc.sync.dma_start(out=out_v[:, t, a, :], in_=o_sb[a, t][:])
+
+        ACC = 5
+
+        interleave_a("V", 0, 0, 0)
+        interleave_a("V", 0, 0, 1, 0, 64)
+        interleave_a("S", 0, 0, 1, 64, 128)
+        turn_x(0, 0, "S")
+        quantize_w("a", 0, 0)
+        turn_x(0, 1, "V")
+        quantize_x(0, 0)
+        interleave_a("V", 1, 0, 0)
+        interleave_a("V", 1, 0, 1, 0, 64)
+        interleave_a("S", 1, 0, 1, 64, 128)
+        quantize_w("a", 1, 0)
+        turn_x(0, 2, "S")
+        turn_x(0, 3, "V")
+        quantize_x(0, 1)
+        for t in range(T):
+            stage1_mm(0, 0, t)
+        for k in range(G):
+            interleave_a("G", k, 1, 0)
+            interleave_a("S", k, 1, 1)
+        c_mid = turn_c("S")
+
+        NS = 2 * A
+        unit = lambda i: (i // 2, i % 2)
+        xturns = {0: [(1, 0), (1, 1)]}
+        for a in range(2, A):
+            xturns[2 * a - 3] = [(a, 0), (a, 1)]
+            xturns[2 * a - 2] = [(a, 2), (a, 3)]
+        for i in range(NS + 3):
+            if i < NS:
+                a, h = unit(i)
+                for t in range(T):
+                    stage1_add(a, h, t)
+                cast_h1(a, h, 0, "S")
+                cast_h1(a, h, 1, "V" if i == 0 else "S")
+            if i == 0:
+                for k in range(G):
+                    quantize_w("a", k, 1)
+            if 3 <= i < NS + 2:
+                quantize_h2(*unit(i - 3))
+            if i == NS + 1:
+                quantize_h2(A - 1, 1)
+            if 1 <= i <= NS:
+                a, h = unit(i - 1)
+                for t in range(T):
+                    stage2_mm(a, h, t)
+                if i == 1:
+                    turn_x(1, 2, "S")
+                    turn_x(1, 3, "S")
+                for t in range(T):
+                    stage2_add(a, h, t)
+            for a, t in xturns.get(i - 1, []):
+                if t % 2 == 1:
+                    quantize_x(a, t // 2)
+            if i in (1, 2):
+                for k in range(G):
+                    quantize_w("b", k, i - 1)
+            if i == 1:
+                quantize_x(1, 1)
+            if i >= 3:
+                a, p = unit(i - 3)
+                for n in range(4):
+                    stage3_mm(a, 2 * p + n // 2, n % 2)
+                    stage3_out(a, 2 * p + n // 2, n % 2, "G" if n in (GOUT if i < NS else GTAIL) else "V")
+            if i + 1 < NS:
+                a, h = unit(i + 1)
+                for t in range(T):
+                    stage1_mm(a, h, t)
+            if i == 0:
+                c_codes.append(quantize(keep, "cq", 1, c_mid[:].rearrange("p t r j -> p (t r j)"), 4 * P))
+            if 2 <= i <= NS:
+                a, p = unit(i - 2)
+                for t in range(2 * p, T if i == NS else 2 * p + 2):
+                    turn_h2(a, t, "S")
+            for a, t in xturns.get(i, []):
+                turn_x(a, t, "S")
+            if i < 2:
+                for k in range(G):
+                    for half in range(2):
+                        interleave_b("G", k, i, half)
+            if i == 1:
+                nc.scalar.copy(out=rate[:], in_=rate_bf[:])
+            if i < NS:
+                quantize_h1(*unit(i))
+
+
+GOUT = (1, 3)
+GTAIL = ()

@@ -83,7 +83,11 @@ def tile_age_gated_labour_flows_t1_kernel(tc, x, switch_a, commute, switch_b, ag
 
         def mid(which, k, h):
             if (which, k, h) not in mid_w:
-                mid_w[which, k, h] = work.tile([P, N, 4], BF16, name="mid_w", tag="mid_w", bufs=3, align_bytes=64)
+                g_own = which == "b" and k == 0
+                if (which, k, h) == ("a", 1, 1):
+                    mid_w[which, k, h] = work.tile([P, N, 4], BF16, name="mid_w", tag="x_mid", bufs=2, align_bytes=64)
+                    return mid_w[which, k, h]
+                mid_w[which, k, h] = work.tile([P, N, 4], BF16, name="mid_w", tag="mid_g" if g_own else "mid_w", bufs=1 if g_own else 3, align_bytes=64)
             return mid_w[which, k, h]
 
         def interleave_a(eng, k, h, u, lo=0, hi=128):
@@ -131,7 +135,7 @@ def tile_age_gated_labour_flows_t1_kernel(tc, x, switch_a, commute, switch_b, ag
 
         def turn_x(a, t, eng):
             if t % 2 == 0:
-                x_mid[a, t // 2] = work.tile([P, 2, G, P, 4], BF16, name="x_mid", bufs=2, align_bytes=64)
+                x_mid[a, t // 2] = work.tile([P, 2, G, P, 4], BF16, name="x_mid", tag="x_mid", bufs=2, align_bytes=64)
             w = x_sb[a][:, t, :].bitcast(F32)
             turn(lambda k, u: w[:, 256 * k + u : 256 * (k + 1) : 2], eng, x_mid[a, t // 2][:, t % 2])
 
@@ -142,7 +146,7 @@ def tile_age_gated_labour_flows_t1_kernel(tc, x, switch_a, commute, switch_b, ag
 
         def turn_c(eng):
             w = c_sb[:].bitcast(F32)
-            m = keep.tile([P, T, P, 4], BF16, name="c_mid", align_bytes=64)
+            m = work.tile([P, T, P, 4], BF16, name="c_mid", tag="mid_g", bufs=1, align_bytes=64)
             for pair in range(2):
                 turn(lambda i, u: w[:, 2 * pair + i, u::2], eng, m[:, 2 * pair : 2 * pair + 2])
             return m
@@ -226,84 +230,128 @@ def tile_age_gated_labour_flows_t1_kernel(tc, x, switch_a, commute, switch_b, ag
         turn_x(0, 0, "S")
         quantize_w("a", 0, 0)
         turn_x(0, 1, "V")
-        quantize_x(0, 0)
         interleave_a("V", 1, 0, 0)
         interleave_a("V", 1, 0, 1, 0, 64)
         interleave_a("S", 1, 0, 1, 64, 128)
+        quantize_x(0, 0)
         quantize_w("a", 1, 0)
         turn_x(0, 2, "S")
-        turn_x(0, 3, "V")
+        turn_x(0, 3, "S")
         quantize_x(0, 1)
         for t in range(T):
             stage1_mm(0, 0, t)
-        for k in range(G):
-            interleave_a("G", k, 1, 0)
-            interleave_a("S", k, 1, 1)
+        interleave_a("S", 0, 1, 1)
+        interleave_a(EA, 0, 1, 0)
+        interleave_a("S", 1, 1, 1)
+        interleave_a("G", 1, 1, 0)
         c_mid = turn_c("S")
 
         NS = 2 * A
         unit = lambda i: (i // 2, i % 2)
-        xturns = {0: [(1, 0), (1, 1)]}
-        for a in range(2, A):
-            xturns[2 * a - 3] = [(a, 0), (a, 1)]
-            xturns[2 * a - 2] = [(a, 2), (a, 3)]
         for i in range(NS + 3):
             if i < NS:
                 a, h = unit(i)
                 for t in range(T):
                     stage1_add(a, h, t)
-                cast_h1(a, h, 0, "S")
-                cast_h1(a, h, 1, "V" if i == 0 else "S")
+                cast_h1(a, h, 0, EC if i == 0 else "S")
+                if i < 3:
+                    cast_h1(a, h, 1, "V" if i == 0 else "S")
             if i == 0:
                 for k in range(G):
                     quantize_w("a", k, 1)
-            if 3 <= i < NS + 2:
+                for t in range(X1):
+                    turn_x(1, t, "S")
+            if 1 <= i <= NS:
+                a, h = unit(i - 1)
+                for t in range(T):
+                    stage2_mm(a, h, t)
+            if 4 <= i <= DL:
+                a, p = unit(i - 4)
+                stage3_mm(a, 2 * p + 1, 0)
+                stage3_out(a, 2 * p + 1, 0, "G")
+            if i in QX_EARLY:
+                quantize_x(*unit(i + 2))
+            if 3 <= i < NS + 1:
                 quantize_h2(*unit(i - 3))
             if i == NS + 1:
                 quantize_h2(A - 1, 1)
             if 1 <= i <= NS:
                 a, h = unit(i - 1)
                 for t in range(T):
-                    stage2_mm(a, h, t)
-                if i == 1:
-                    turn_x(1, 2, "S")
-                    turn_x(1, 3, "S")
-                for t in range(T):
                     stage2_add(a, h, t)
-            for a, t in xturns.get(i - 1, []):
-                if t % 2 == 1:
-                    quantize_x(a, t // 2)
-            if i in (1, 2):
-                for k in range(G):
-                    quantize_w("b", k, i - 1)
+                    if t == 0 and 4 <= i <= DL:
+                        b, p = unit(i - 4)
+                        stage3_mm(b, 2 * p + 1, 1)
+                        stage3_out(b, 2 * p + 1, 1, "G")
+            if i == 2 and BV2 == "V":
+                interleave_b("V", 1, 1, 1)
+            if i == 1 and BV1 == "V":
+                interleave_b("V", 1, 0, 1)
             if i == 1:
+                quantize_x(1, 0)
                 quantize_x(1, 1)
+            if i in (1, 2):
+                quantize_w("b", 1, i - 1)
             if i >= 3:
                 a, p = unit(i - 3)
                 for n in range(4):
-                    stage3_mm(a, 2 * p + n // 2, n % 2)
-                    stage3_out(a, 2 * p + n // 2, n % 2, "G" if n in (GOUT if i < NS else GTAIL) else "V")
+                    if not (i < DL and n >= 2):
+                        stage3_mm(a, 2 * p + n // 2, n % 2)
+                        stage3_out(a, 2 * p + n // 2, n % 2, "G" if i == NS and n in GT8 else "V")
+                    if i == NS and n == TA:
+                        turn_h2(A - 1, 0, "S")
+                        turn_h2(A - 1, 1, "S")
+                    if i == NS and n == TB:
+                        turn_h2(A - 1, 2, "S")
+                        turn_h2(A - 1, 3, "S")
+                    if i == NS and n == QA:
+                        quantize_h2(A - 1, 0)
+                if i < NS:
+                    cast_h1(*unit(i), 1, "S")
             if i + 1 < NS:
                 a, h = unit(i + 1)
                 for t in range(T):
                     stage1_mm(a, h, t)
-            if i == 0:
-                c_codes.append(quantize(keep, "cq", 1, c_mid[:].rearrange("p t r j -> p (t r j)"), 4 * P))
-            if 2 <= i <= NS:
+            if 2 <= i < NS:
                 a, p = unit(i - 2)
-                for t in range(2 * p, T if i == NS else 2 * p + 2):
+                for t in range(2 * p, 2 * p + 2):
                     turn_h2(a, t, "S")
-            for a, t in xturns.get(i, []):
-                turn_x(a, t, "S")
-            if i < 2:
-                for k in range(G):
-                    for half in range(2):
-                        interleave_b("G", k, i, half)
+            if i == 0:
+                for t in range(X1, T):
+                    turn_x(1, t, "S")
+                interleave_b("S", 1, 0, 0)
+                if BV1 == "S":
+                    interleave_b("S", 1, 0, 1)
+            if i == 1:
+                interleave_b("S", 1, 1, 0)
+                if BV2 == "S":
+                    interleave_b("S", 1, 1, 1)
+            if 1 <= i <= 4:
+                a, p = unit(i + 3)
+                turn_x(a, 2 * p, "S")
+                turn_x(a, 2 * p + 1, "S")
             if i == 1:
                 nc.scalar.copy(out=rate[:], in_=rate_bf[:])
+            if i in QX_LATE:
+                quantize_x(*unit(i + 2))
             if i < NS:
                 quantize_h1(*unit(i))
+            if i == 0:
+                c_codes.append(quantize(keep, "cq", 1, c_mid[:].rearrange("p t r j -> p (t r j)"), 4 * P))
+            if i in (1, 2):
+                quantize_w("b", 0, i - 1)
+            if i < 2:
+                for half in range(2):
+                    interleave_b("G", 0, i, half)
 
 
-GOUT = (1, 3)
-GTAIL = ()
+QX_EARLY = (3, 5)
+QX_LATE = (2, 4)
+DL = 7
+GT8 = ()
+TA, TB, QA = 1, 3, 1
+EA = "S"
+EC = "V"
+X1 = 4
+BV1 = "S"
+BV2 = "S"

@@ -60,10 +60,11 @@ def tile_age_gated_labour_flows_t1_kernel(tc, x, switch_a, commute, switch_b, ag
         c_sb = keep.tile([P, T, R], BF16, name="c_sb")
         nc.sync.dma_start(out=c_sb[:], in_=commute.rearrange("(p t) i -> p t i", t=T))
         load_x(1, 1, 0)
-        for h in range(2):
-            for k in range(G):
-                load_w(switch_b, "b", k, h)
+        for k in range(G):
+            load_w(switch_b, "b", k, 0)
         load_x(2, 1, 0)
+        for k in range(G):
+            load_w(switch_b, "b", k, 1)
         rate_bf = keep.tile([P, T], BF16, name="rate_bf")
         nc.sync.dma_start(out=rate_bf[:], in_=region_rate.rearrange("(p t) -> p t", t=T))
         gate = keep.tile([P, A, O], BF16, name="gate")
@@ -85,7 +86,7 @@ def tile_age_gated_labour_flows_t1_kernel(tc, x, switch_a, commute, switch_b, ag
             if (which, k, h) not in mid_w:
                 g_own = which == "b" and k == 0
                 if (which, k, h) == ("a", 1, 1):
-                    mid_w[which, k, h] = work.tile([P, N, 4], BF16, name="mid_w", tag="x_mid", bufs=2, align_bytes=64)
+                    mid_w[which, k, h] = work.tile([P, N, 4], BF16, name="mid_w", tag="x_mid", bufs=3, align_bytes=64)
                     return mid_w[which, k, h]
                 mid_w[which, k, h] = work.tile([P, N, 4], BF16, name="mid_w", tag="mid_g" if g_own else "mid_w", bufs=1 if g_own else 3, align_bytes=64)
             return mid_w[which, k, h]
@@ -135,7 +136,7 @@ def tile_age_gated_labour_flows_t1_kernel(tc, x, switch_a, commute, switch_b, ag
 
         def turn_x(a, t, eng):
             if t % 2 == 0:
-                x_mid[a, t // 2] = work.tile([P, 2, G, P, 4], BF16, name="x_mid", tag="x_mid", bufs=2, align_bytes=64)
+                x_mid[a, t // 2] = work.tile([P, 2, G, P, 4], BF16, name="x_mid", tag="x_mid", bufs=3, align_bytes=64)
             w = x_sb[a][:, t, :].bitcast(F32)
             turn(lambda k, u: w[:, 256 * k + u : 256 * (k + 1) : 2], eng, x_mid[a, t // 2][:, t % 2])
 
@@ -214,10 +215,10 @@ def tile_age_gated_labour_flows_t1_kernel(tc, x, switch_a, commute, switch_b, ag
             if eng == "V":
                 nc.vector.scalar_tensor_tensor(out=o, in0=acc[:], scalar=rate[:, t : t + 1], in1=g, op0=MULT, op1=MULT)
             else:
-                tmp = work.tile([P, N], F32, name="tmp", bufs=2)
+                tmp = work.tile([P, N], F32, name="tmp", bufs=3)
                 nc.scalar.activation(out=tmp[:], in_=acc[:], func=COPY, scale=rate[:, t : t + 1])
                 nc.gpsimd.tensor_tensor(out=o, in0=tmp[:], in1=g, op=MULT)
-            if a == A - 1:
+            if a == A - 1 and t >= FS:
                 nc.sync.dma_start(out=out_v[:, t, a, h * N : (h + 1) * N], in_=o)
             elif h == 1:
                 nc.sync.dma_start(out=out_v[:, t, a, :], in_=o_sb[a, t][:])
@@ -250,108 +251,91 @@ def tile_age_gated_labour_flows_t1_kernel(tc, x, switch_a, commute, switch_b, ag
         unit = lambda i: (i // 2, i % 2)
         for i in range(NS + 3):
             if i < NS:
-                a, h = unit(i)
                 for t in range(T):
-                    stage1_add(a, h, t)
-                cast_h1(a, h, 0, EC if i == 0 else "S")
-                if i < 3:
-                    cast_h1(a, h, 1, "V" if i == 0 else "S")
+                    stage1_add(*unit(i), t)
+            if 3 <= i <= NS:
+                a, p = unit(i - 3)
+                turn_h2(a, 2 * p, "S")
+                turn_h2(a, 2 * p + 1, "S")
             if i == 0:
+                cast_h1(0, 0, 0, EC)
+                cast_h1(0, 0, 1, "V")
                 for k in range(G):
                     quantize_w("a", k, 1)
-                for t in range(X1):
-                    turn_x(1, t, "S")
-            if 1 <= i <= NS:
-                a, h = unit(i - 1)
-                for t in range(T):
-                    stage2_mm(a, h, t)
-            if 4 <= i <= DL:
-                a, p = unit(i - 4)
-                stage3_mm(a, 2 * p + 1, 0)
-                stage3_out(a, 2 * p + 1, 0, "G")
-            if i in QX_EARLY:
-                quantize_x(*unit(i + 2))
-            if 3 <= i < NS + 1:
-                quantize_h2(*unit(i - 3))
-            if i == NS + 1:
-                quantize_h2(A - 1, 1)
-            if 1 <= i <= NS:
-                a, h = unit(i - 1)
-                for t in range(T):
-                    stage2_add(a, h, t)
-                    if t == 0 and 4 <= i <= DL:
-                        b, p = unit(i - 4)
-                        stage3_mm(b, 2 * p + 1, 1)
-                        stage3_out(b, 2 * p + 1, 1, "G")
-            if i == 2 and BV2 == "V":
-                interleave_b("V", 1, 1, 1)
-            if i == 1 and BV1 == "V":
-                interleave_b("V", 1, 0, 1)
-            if i == 1:
-                quantize_x(1, 0)
-                quantize_x(1, 1)
-            if i in (1, 2):
-                quantize_w("b", 1, i - 1)
-            if i >= 3:
-                a, p = unit(i - 3)
-                for n in range(4):
-                    if not (i < DL and n >= 2):
-                        stage3_mm(a, 2 * p + n // 2, n % 2)
-                        stage3_out(a, 2 * p + n // 2, n % 2, "G" if i == NS and n in GT8 else "V")
-                    if i == NS and n == TA:
-                        turn_h2(A - 1, 0, "S")
-                        turn_h2(A - 1, 1, "S")
-                    if i == NS and n == TB:
-                        turn_h2(A - 1, 2, "S")
-                        turn_h2(A - 1, 3, "S")
-                    if i == NS and n == QA:
-                        quantize_h2(A - 1, 0)
-                if i < NS:
-                    cast_h1(*unit(i), 1, "S")
-            if i + 1 < NS:
-                a, h = unit(i + 1)
-                for t in range(T):
-                    stage1_mm(a, h, t)
-            if 2 <= i < NS:
-                a, p = unit(i - 2)
-                for t in range(2 * p, 2 * p + 2):
-                    turn_h2(a, t, "S")
             if i == 0:
-                for t in range(X1, T):
+                for t in range(T):
                     turn_x(1, t, "S")
-                interleave_b("S", 1, 0, 0)
-                if BV1 == "S":
-                    interleave_b("S", 1, 0, 1)
-            if i == 1:
-                interleave_b("S", 1, 1, 0)
-                if BV2 == "S":
-                    interleave_b("S", 1, 1, 1)
-            if 1 <= i <= 4:
+            if 2 <= i < NS - 3:
                 a, p = unit(i + 3)
                 turn_x(a, 2 * p, "S")
                 turn_x(a, 2 * p + 1, "S")
-            if i == 1:
-                nc.scalar.copy(out=rate[:], in_=rate_bf[:])
-            if i in QX_LATE:
-                quantize_x(*unit(i + 2))
-            if i < NS:
-                quantize_h1(*unit(i))
             if i == 0:
                 c_codes.append(quantize(keep, "cq", 1, c_mid[:].rearrange("p t r j -> p (t r j)"), 4 * P))
+            if 1 <= i <= NS:
+                quantize_h1(*unit(i - 1))
+                for t in range(T):
+                    stage2_mm(*unit(i - 1), t)
+            if i == 1:
+                cast_h1(0, 1, 0, "S")
+                cast_h1(0, 1, 1, "S")
+                turn_x(2, 0, "S")
+                turn_x(2, 1, "S")
+                quantize_x(1, 0)
+            if 1 <= i < NS - 2:
+                quantize_x(*unit(i + 2))
+            if 3 <= i <= NS:
+                quantize_h2(*unit(i - 3))
             if i in (1, 2):
-                quantize_w("b", 0, i - 1)
-            if i < 2:
+                for k in range(G):
+                    quantize_w("b", k, i - 1)
+            if i == 0:
                 for half in range(2):
-                    interleave_b("G", 0, i, half)
+                    interleave_b("S", 1, 0, half)
+                    interleave_b("G", 0, 0, half)
+            if i == 1:
+                for half in range(2):
+                    interleave_b("S", 1, 1, half)
+                    interleave_b("G", 0, 1, half)
+                nc.scalar.copy(out=rate[:], in_=rate_bf[:])
+            if 2 <= i < NS:
+                cast_h1(*unit(i), 0, "S")
+            if 1 <= i <= NS:
+                for t in range(T):
+                    stage2_add(*unit(i - 1), t)
+            if i == 2:
+                cast_h1(*unit(i), 1, "S")
+            if i >= 3:
+                a, p = unit(i - 3)
+                for n in range(4):
+                    stage3_mm(a, 2 * p + n // 2, n % 2)
+                    stage3_out(a, 2 * p + n // 2, n % 2, "G" if n in (GO if i < NS - 1 else GO7 if i < NS else GT8 if i == NS else GT9 if i == NS + 1 else GT10) else "V")
+                    if i == NS and n == TA:
+                        turn_h2(A - 1, 0, "S")
+                        turn_h2(A - 1, 1, E1)
+                    if i == NS and n == TB:
+                        turn_h2(A - 1, 2, "S")
+                        turn_h2(A - 1, 3, E3)
+                    if i == NS and n == QA:
+                        quantize_h2(A - 1, 0)
+                    if i == NS + 1 and n == QB:
+                        quantize_h2(A - 1, 1)
+                    if 3 <= i < NS and n == CN:
+                        cast_h1(*unit(i), 1, "S")
+            if i + 1 < NS:
+                for t in range(T):
+                    stage1_mm(*unit(i + 1), t)
 
 
-QX_EARLY = (3, 5)
-QX_LATE = (2, 4)
-DL = 7
-GT8 = ()
+GO7 = (0,)
+E1 = "S"
+E3 = "S"
+QB = 0
+GT9 = ()
+GT10 = ()
+FS = 0
+GT8 = (0, 2)
 TA, TB, QA = 1, 3, 1
 EA = "S"
 EC = "V"
-X1 = 4
-BV1 = "S"
-BV2 = "S"
+GO = (0, 1, 2)
+CN = 3

@@ -63,13 +63,13 @@ def tile_age_gated_labour_flows_t1_kernel(tc, x, switch_a, commute, switch_b, ag
         for k in range(G):
             load_w(switch_b, "b", k, 0)
         load_x(2, 1, 0)
+        load_x(3, 1, 0)
         for k in range(G):
             load_w(switch_b, "b", k, 1)
         rate_bf = keep.tile([P, T], BF16, name="rate_bf")
         nc.sync.dma_start(out=rate_bf[:], in_=region_rate.rearrange("(p t) -> p t", t=T))
         gate = keep.tile([P, A, O], BF16, name="gate")
         nc.sync.dma_start(out=gate[:], in_=age_gate.partition_broadcast(P))
-        load_x(3, 1, 0)
         rate = keep.tile([P, T], F32, name="rate")
 
         mid_w = {}
@@ -218,7 +218,7 @@ def tile_age_gated_labour_flows_t1_kernel(tc, x, switch_a, commute, switch_b, ag
                 tmp = work.tile([P, N], F32, name="tmp", bufs=3)
                 nc.scalar.activation(out=tmp[:], in_=acc[:], func=COPY, scale=rate[:, t : t + 1])
                 nc.gpsimd.tensor_tensor(out=o, in0=tmp[:], in1=g, op=MULT)
-            if a == A - 1 and t >= FS:
+            if a == A - 1:
                 nc.sync.dma_start(out=out_v[:, t, a, h * N : (h + 1) * N], in_=o)
             elif h == 1:
                 nc.sync.dma_start(out=out_v[:, t, a, :], in_=o_sb[a, t][:])
@@ -251,91 +251,104 @@ def tile_age_gated_labour_flows_t1_kernel(tc, x, switch_a, commute, switch_b, ag
         unit = lambda i: (i // 2, i % 2)
         for i in range(NS + 3):
             if i < NS:
-                for t in range(T):
+                for t in range(LATE if i else T):
                     stage1_add(*unit(i), t)
             if 3 <= i <= NS:
                 a, p = unit(i - 3)
                 turn_h2(a, 2 * p, "S")
                 turn_h2(a, 2 * p + 1, "S")
-            if i == 0:
-                cast_h1(0, 0, 0, EC)
-                cast_h1(0, 0, 1, "V")
-                for k in range(G):
-                    quantize_w("a", k, 1)
-            if i == 0:
-                for t in range(T):
-                    turn_x(1, t, "S")
-            if 2 <= i < NS - 3:
-                a, p = unit(i + 3)
-                turn_x(a, 2 * p, "S")
-                turn_x(a, 2 * p + 1, "S")
-            if i == 0:
-                c_codes.append(quantize(keep, "cq", 1, c_mid[:].rearrange("p t r j -> p (t r j)"), 4 * P))
+            for a, t in XL.get(i, ()):
+                turn_x(a, t, "S")
+            if 2 <= i < NS:
+                for t in range(LATE, T):
+                    stage1_mm(*unit(i), t)
             if 1 <= i <= NS:
                 quantize_h1(*unit(i - 1))
+            if 1 <= i < NS:
+                for t in range(LATE, T):
+                    stage1_add(*unit(i), t)
+            if i == 0:
+                for k in range(G):
+                    quantize_w("a", k, 1)
+                for t in range(T):
+                    stage1_mm(0, 1, t)
+                cast_h1(0, 0, 0, EC)
+                cast_h1(0, 0, 1, "V")
+                c_codes.append(quantize(keep, "cq", 1, c_mid[:].rearrange("p t r j -> p (t r j)"), 4 * P))
+                for half in range(NB):
+                    interleave_b("S", 1, 0, half)
+                for half in range(2):
+                    interleave_b("G", 0, 0, half)
+                for t in range(T):
+                    turn_x(1, t, "S")
+            if 1 <= i <= NS:
                 for t in range(T):
                     stage2_mm(*unit(i - 1), t)
             if i == 1:
                 cast_h1(0, 1, 0, "S")
                 cast_h1(0, 1, 1, "S")
-                turn_x(2, 0, "S")
-                turn_x(2, 1, "S")
-                quantize_x(1, 0)
-            if 1 <= i < NS - 2:
-                quantize_x(*unit(i + 2))
+                for half in range(NB, 2):
+                    interleave_b("S", 1, 0, half)
+            if i not in AFTER:
+                for a, p in QX.get(i, ()):
+                    quantize_x(a, p)
+            for a, t in XE.get(i, ()):
+                turn_x(a, t, "S")
             if 3 <= i <= NS:
                 quantize_h2(*unit(i - 3))
-            if i in (1, 2):
+            if i == 2 and i not in AFTER:
                 for k in range(G):
-                    quantize_w("b", k, i - 1)
-            if i == 0:
-                for half in range(2):
-                    interleave_b("S", 1, 0, half)
-                    interleave_b("G", 0, 0, half)
-            if i == 1:
-                for half in range(2):
-                    interleave_b("S", 1, 1, half)
-                    interleave_b("G", 0, 1, half)
-                nc.scalar.copy(out=rate[:], in_=rate_bf[:])
+                    quantize_w("b", k, 1)
             if 2 <= i < NS:
                 cast_h1(*unit(i), 0, "S")
             if 1 <= i <= NS:
                 for t in range(T):
                     stage2_add(*unit(i - 1), t)
+            if i in AFTER:
+                for a, p in QX.get(i, ()):
+                    quantize_x(a, p)
+                for k in range(G):
+                    quantize_w("b", k, i - 1)
+            if i == 1:
+                for half in range(2):
+                    interleave_b("S", 1, 1, half)
+                    interleave_b("G", 0, 1, half)
+                nc.scalar.copy(out=rate[:], in_=rate_bf[:])
             if i == 2:
                 cast_h1(*unit(i), 1, "S")
             if i >= 3:
                 a, p = unit(i - 3)
                 for n in range(4):
                     stage3_mm(a, 2 * p + n // 2, n % 2)
-                    stage3_out(a, 2 * p + n // 2, n % 2, "G" if n in (GO if i < NS - 1 else GO7 if i < NS else GT8 if i == NS else GT9 if i == NS + 1 else GT10) else "V")
+                    stage3_out(a, 2 * p + n // 2, n % 2, "G" if n in (GO if i < NS - 1 else GO7 if i < NS else GT8 if i == NS else ()) else "V")
                     if i == NS and n == TA:
                         turn_h2(A - 1, 0, "S")
-                        turn_h2(A - 1, 1, E1)
+                        turn_h2(A - 1, 1, "S")
                     if i == NS and n == TB:
                         turn_h2(A - 1, 2, "S")
-                        turn_h2(A - 1, 3, E3)
+                        turn_h2(A - 1, 3, "S")
                     if i == NS and n == QA:
                         quantize_h2(A - 1, 0)
                     if i == NS + 1 and n == QB:
                         quantize_h2(A - 1, 1)
                     if 3 <= i < NS and n == CN:
                         cast_h1(*unit(i), 1, "S")
-            if i + 1 < NS:
-                for t in range(T):
+            if 1 <= i < NS - 1:
+                for t in range(LATE):
                     stage1_mm(*unit(i + 1), t)
 
 
+QX = {1: [(1, 0), (1, 1)], 2: [(2, 0), (2, 1)], 3: [(3, 0)], 4: [(3, 1)]}
+XE = {1: [(2, 0), (2, 1)], 2: [(3, 0), (3, 1)], 3: [(3, 2), (3, 3)]}
+XL = {2: [(2, 2), (2, 3)]}
+AFTER = (1,)
+NB = 1
 GO7 = (0,)
-E1 = "S"
-E3 = "S"
 QB = 0
-GT9 = ()
-GT10 = ()
-FS = 0
-GT8 = (0, 2)
+LATE = 3
+GT8 = ()
 TA, TB, QA = 1, 3, 1
 EA = "S"
-EC = "V"
-GO = (0, 1, 2)
+EC = "S"
+GO = (0, 1)
 CN = 3

from contextlib import ExitStack

import concourse.mybir as mybir
from concourse.masks import make_identity

R, A, O = 512, 4, 1024
FLOPS = 2 * R * A * O * O * 2 + 2 * R * R * A * O

F32 = mybir.dt.float32
BF16 = mybir.dt.bfloat16
U32 = mybir.dt.uint32
U8 = mybir.dt.uint8
FP8X4 = mybir.dt.float8_e4m3fn_x4
ADD = mybir.AluOpType.add
MULT = mybir.AluOpType.mult
COPY = mybir.ActivationFunctionType.Copy

P = 128
T = 4
N = 512
G = O // 512


def tile_age_gated_labour_flows_t1_kernel(tc, x, switch_a, commute, switch_b, age_gate, region_rate, out):
    nc = tc.nc
    x_v = x.rearrange("(p t) a o -> p t a o", t=T)
    out_v = out.rearrange("(p t) a o -> p t a o", t=T)

    with ExitStack() as ctx:
        keep = ctx.enter_context(tc.tile_pool(name="keep", bufs=1))
        work = ctx.enter_context(tc.tile_pool(name="work", bufs=2))
        psum = ctx.enter_context(tc.psum_pool(name="psum", bufs=1))
        ctx.enter_context(tc.manual_schedule())

        x_sb, raw_w, codes_w = {}, {}, {}

        def load_x(a, pieces, i):
            if i == 0:
                x_sb[a] = keep.tile([P, T, O], BF16, name=f"x{a}")
            ts = slice(i * T // pieces, (i + 1) * T // pieces)
            nc.sync.dma_start(out=x_sb[a][:, ts, :], in_=x_v[:, ts, a, :])

        def load_w(w, which, k, h):
            t = keep.tile([P, 4, N], BF16, name=f"raw_{which}{k}{h}")
            nc.sync.dma_start(
                out=t[:],
                in_=w[k * 512 : (k + 1) * 512, h * N : (h + 1) * N].rearrange("(p j) o -> p j o", j=4),
            )
            raw_w[which, k, h] = t

        ident = keep.tile([P, P], F32, name="ident")
        make_identity(nc, ident[:])

        load_w(switch_a, "a", 0, 0)
        load_x(0, 2, 0)
        load_w(switch_a, "a", 1, 0)
        load_x(0, 2, 1)
        load_w(switch_a, "a", 0, 1)
        load_w(switch_a, "a", 1, 1)
        c_sb = keep.tile([P, T, R], BF16, name="c_sb")
        nc.sync.dma_start(out=c_sb[:], in_=commute.rearrange("(p t) i -> p t i", t=T))
        load_x(1, 1, 0)
        for k in range(G):
            load_w(switch_b, "b", k, 0)
        load_x(2, 1, 0)
        load_x(3, 1, 0)
        for k in range(G):
            load_w(switch_b, "b", k, 1)
        rate_bf = keep.tile([P, T], BF16, name="rate_bf")
        nc.sync.dma_start(out=rate_bf[:], in_=region_rate.rearrange("(p t) -> p t", t=T))
        gate = keep.tile([P, A, O], BF16, name="gate")
        nc.sync.dma_start(out=gate[:], in_=age_gate.partition_broadcast(P))
        rate = keep.tile([P, T], F32, name="rate")

        mid_w = {}

        def copy_on(eng, out, in_):
            if eng == "V":
                nc.vector.tensor_copy(out=out, in_=in_)
            elif eng == "S":
                nc.scalar.copy(out=out, in_=in_)
            else:
                nc.gpsimd.tensor_scalar(out=out, in0=in_, scalar1=1.0, scalar2=0.0, op0=MULT, op1=ADD)

        def mid(which, k, h):
            if (which, k, h) not in mid_w:
                g_own = which == "b" and k == 0
                if (which, k, h) == ("a", 1, 1):
                    mid_w[which, k, h] = work.tile([P, N, 4], BF16, name="mid_w", tag="x_mid", bufs=3, align_bytes=64)
                    return mid_w[which, k, h]
                mid_w[which, k, h] = work.tile([P, N, 4], BF16, name="mid_w", tag="mid_g" if g_own else "mid_w", bufs=1 if g_own else 3, align_bytes=64)
            return mid_w[which, k, h]

        def interleave_a(eng, k, h, u, lo=0, hi=128):
            raw = raw_w["a", k, h][:].rearrange("p j (q u e) -> p u q e j", u=2, e=2)[:, u, lo:hi]
            dst = mid("a", k, h)[:].rearrange("p (u q e) j -> p u q e j", u=2, e=2)[:, u, lo:hi]
            copy_on(eng, dst, raw)

        def interleave_b(eng, k, h, half):
            cols = slice(half * 256, half * 256 + 256)
            copy_on(eng, mid("b", k, h)[:, cols, :], raw_w["b", k, h][:, :, cols].rearrange("p j n -> p n j"))

        def quantize(pool, name, bufs, src, width):
            c = pool.tile([P, width], U32, name=name + "_c", tag=name + "_c", bufs=bufs, align_bytes=64)
            s = pool.tile([P, width], U8, name=name + "_s", tag=name + "_s", bufs=bufs, align_bytes=64)
            nc.vector.quantize_mx(out=c[:].bitcast(FP8X4), scales=s[:], in_=src)
            return c, s

        def quantize_w(which, k, h):
            codes_w[which, k, h] = quantize(
                keep, f"w{which}{k}{h}", 1, mid(which, k, h)[:].rearrange("p n j -> p (n j)"), N
            )

        def mm(acc, lhs, lcols, rhs, k, first, last):
            nc.tensor.matmul_mx(
                out=acc[:],
                lhsT=lhs[0][:, lcols].bitcast(FP8X4),
                lhsT_scale=lhs[1][:, lcols],
                rhs=rhs[0][:].bitcast(FP8X4),
                rhs_scale=rhs[1][:],
                start=first,
                stop=last,
            )

        def acc_tile():
            return psum.tile([P, N], F32, name="acc", tag="acc", bufs=ACC)

        def turn(words, eng, dst):
            tr = psum.tile([P, 2, 2, P], F32, name="tr", tag="tr", bufs=8 - ACC)
            for i in range(2):
                for u in range(2):
                    nc.tensor.transpose(tr[:, i, u, :], words(i, u), ident[:])
            copy_on(eng, dst.bitcast(F32), tr[:].rearrange("p i u r -> p i r u"))

        x_mid, x_codes = {}, {}

        def turn_x(a, t, eng):
            if t % 2 == 0:
                x_mid[a, t // 2] = work.tile([P, 2, G, P, 4], BF16, name="x_mid", tag="x_mid", bufs=3, align_bytes=64)
            w = x_sb[a][:, t, :].bitcast(F32)
            turn(lambda k, u: w[:, 256 * k + u : 256 * (k + 1) : 2], eng, x_mid[a, t // 2][:, t % 2])

        def quantize_x(a, pair):
            x_codes[a, pair] = quantize(work, "x", 4, x_mid[a, pair][:].rearrange("p t k r j -> p (t k r j)"), 4 * P)

        c_codes = []

        def turn_c(eng):
            w = c_sb[:].bitcast(F32)
            m = work.tile([P, T, P, 4], BF16, name="c_mid", tag="mid_g", bufs=1, align_bytes=64)
            for pair in range(2):
                turn(lambda i, u: w[:, 2 * pair + i, u::2], eng, m[:, 2 * pair : 2 * pair + 2])
            return m

        h1, h1_mid, h1_codes, h2 = {}, {}, {}, {}
        acc1, acc2, acc3 = {}, {}, {}

        def stage1_mm(a, h, t):
            acc1[a, h, t] = acc = acc_tile()
            for k in range(G):
                mm(acc, x_codes[a, t // 2], slice(((t % 2) * G + k) * P, ((t % 2) * G + k + 1) * P), codes_w["a", k, h], k, k == 0, k == G - 1)

        def stage1_add(a, h, t):
            if t == 0:
                h1[a, h] = work.tile([P, T, N], F32, name="h1", bufs=3)
            nc.vector.tensor_tensor(
                out=h1[a, h][:, t, :].rearrange("p (u q e) -> p u q e", u=2, e=2),
                in0=acc1[a, h, t][:].rearrange("p (u q e) -> p u q e", u=2, e=2),
                in1=x_sb[a][:, t, h * N : (h + 1) * N].rearrange("p (q u e) -> p u q e", u=2, e=2),
                op=ADD,
            )

        def cast_h1(a, h, half, eng):
            if half == 0:
                h1_mid[a, h] = work.tile([P, N, T], BF16, name="h1_mid", bufs=2, align_bytes=64)
            cols = slice(half * 256, half * 256 + 256)
            copy_on(eng, h1_mid[a, h][:, cols, :], h1[a, h][:, :, cols].rearrange("p t n -> p n t"))

        def quantize_h1(a, h):
            h1_codes[a, h] = quantize(work, "h1q", 2, h1_mid[a, h][:].rearrange("p n t -> p (n t)"), N)

        def stage2_mm(a, h, t):
            acc2[a, h, t] = acc = acc_tile()
            mm(acc, c_codes[0], slice(t * P, (t + 1) * P), h1_codes[a, h], 0, True, True)

        def stage2_add(a, h, t):
            if h == 0:
                h2[a, t] = work.tile([P, O], BF16, name="h2", bufs=8)
            nc.vector.tensor_tensor(
                out=h2[a, t][:, h * N : (h + 1) * N], in0=acc2[a, h, t][:], in1=h1[a, h][:, t, :], op=ADD
            )

        h2_mid, h2_codes, o_sb = {}, {}, {}

        def turn_h2(a, t, eng):
            if t % 2 == 0:
                h2_mid[a, t // 2] = work.tile([P, 2, G, P, 4], BF16, name="h2_mid", bufs=2, align_bytes=64)
            w = h2[a, t][:].bitcast(F32)
            turn(lambda k, u: w[:, (2 * k + u) * P : (2 * k + u + 1) * P], eng, h2_mid[a, t // 2][:, t % 2])

        def quantize_h2(a, pair):
            h2_codes[a, pair] = quantize(work, "h2q", 4, h2_mid[a, pair][:].rearrange("p t k r j -> p (t k r j)"), 4 * P)

        def stage3_mm(a, t, h):
            acc3[a, t, h] = acc = acc_tile()
            for k in range(G):
                mm(acc, h2_codes[a, t // 2], slice(((t % 2) * G + k) * P, ((t % 2) * G + k + 1) * P), codes_w["b", k, h], k, k == 0, k == G - 1)

        def stage3_out(a, t, h, eng):
            if h == 0:
                o_sb[a, t] = work.tile([P, O], F32, name="o_sb", bufs=5)
            acc = acc3[a, t, h]
            o = o_sb[a, t][:, h * N : (h + 1) * N]
            g = gate[:, a, h * N : (h + 1) * N]
            if eng == "V":
                nc.vector.scalar_tensor_tensor(out=o, in0=acc[:], scalar=rate[:, t : t + 1], in1=g, op0=MULT, op1=MULT)
            else:
                tmp = work.tile([P, N], F32, name="tmp", bufs=3)
                nc.scalar.activation(out=tmp[:], in_=acc[:], func=COPY, scale=rate[:, t : t + 1])
                nc.gpsimd.tensor_tensor(out=o, in0=tmp[:], in1=g, op=MULT)
            if a == A - 1:
                nc.sync.dma_start(out=out_v[:, t, a, h * N : (h + 1) * N], in_=o)
            elif h == 1:
                nc.sync.dma_start(out=out_v[:, t, a, :], in_=o_sb[a, t][:])

        ACC = 5

        interleave_a("V", 0, 0, 0)
        interleave_a("V", 0, 0, 1, 0, 64)
        interleave_a("S", 0, 0, 1, 64, 128)
        turn_x(0, 0, "S")
        quantize_w("a", 0, 0)
        turn_x(0, 1, "V")
        interleave_a("V", 1, 0, 0)
        interleave_a("V", 1, 0, 1, 0, 64)
        interleave_a("S", 1, 0, 1, 64, 128)
        quantize_x(0, 0)
        quantize_w("a", 1, 0)
        turn_x(0, 2, "S")
        turn_x(0, 3, "S")
        quantize_x(0, 1)
        for t in range(T):
            stage1_mm(0, 0, t)
        interleave_a("S", 0, 1, 1)
        interleave_a(EA, 0, 1, 0)
        interleave_a("S", 1, 1, 1)
        interleave_a("G", 1, 1, 0)
        c_mid = turn_c("S")

        NS = 2 * A
        unit = lambda i: (i // 2, i % 2)
        for i in range(NS + 3):
            if i < NS:
                for t in range(LATE if i else T):
                    stage1_add(*unit(i), t)
            if 3 <= i <= NS:
                a, p = unit(i - 3)
                turn_h2(a, 2 * p, "S")
                turn_h2(a, 2 * p + 1, "S")
            for a, t in XL.get(i, ()):
                turn_x(a, t, "S")
            if 2 <= i < NS:
                for t in range(LATE, T):
                    stage1_mm(*unit(i), t)
            if 1 <= i <= NS:
                quantize_h1(*unit(i - 1))
            if 1 <= i < NS:
                for t in range(LATE, T):
                    stage1_add(*unit(i), t)
            if i == 0:
                for k in range(G):
                    quantize_w("a", k, 1)
                for t in range(T):
                    stage1_mm(0, 1, t)
                cast_h1(0, 0, 0, EC)
                cast_h1(0, 0, 1, "V")
                c_codes.append(quantize(keep, "cq", 1, c_mid[:].rearrange("p t r j -> p (t r j)"), 4 * P))
                for half in range(NB):
                    interleave_b("S", 1, 0, half)
                for half in range(2):
                    interleave_b("G", 0, 0, half)
                for t in range(T):
                    turn_x(1, t, "S")
            if 1 <= i <= NS:
                for t in range(T):
                    stage2_mm(*unit(i - 1), t)
            if i == 1:
                cast_h1(0, 1, 0, "S")
                cast_h1(0, 1, 1, "S")
                for half in range(NB, 2):
                    interleave_b("S", 1, 0, half)
            if i not in AFTER:
                for a, p in QX.get(i, ()):
                    quantize_x(a, p)
            for a, t in XE.get(i, ()):
                turn_x(a, t, "S")
            if 3 <= i <= NS:
                quantize_h2(*unit(i - 3))
            if i == 2 and i not in AFTER:
                for k in range(G):
                    quantize_w("b", k, 1)
            if 2 <= i < NS:
                cast_h1(*unit(i), 0, "S")
            if 1 <= i <= NS:
                for t in range(T):
                    stage2_add(*unit(i - 1), t)
            if i in AFTER:
                for a, p in QX.get(i, ()):
                    quantize_x(a, p)
                for k in range(G):
                    quantize_w("b", k, i - 1)
            if i == 1:
                for half in range(2):
                    interleave_b("S", 1, 1, half)
                    interleave_b("G", 0, 1, half)
                nc.scalar.copy(out=rate[:], in_=rate_bf[:])
            if i == 2:
                cast_h1(*unit(i), 1, "S")
            if i >= 3:
                a, p = unit(i - 3)
                for n in range(4):
                    stage3_mm(a, 2 * p + n // 2, n % 2)
                    stage3_out(a, 2 * p + n // 2, n % 2, "G" if n in (GO if i < NS - 1 else GO7 if i < NS else GT8 if i == NS else ()) else "V")
                    if i == NS and n == TA:
                        turn_h2(A - 1, 0, "S")
                        turn_h2(A - 1, 1, "S")
                    if i == NS and n == TB:
                        turn_h2(A - 1, 2, "S")
                        turn_h2(A - 1, 3, "S")
                    if i == NS and n == QA:
                        quantize_h2(A - 1, 0)
                    if i == NS + 1 and n == QB:
                        quantize_h2(A - 1, 1)
                    if 3 <= i < NS and n == CN:
                        cast_h1(*unit(i), 1, "S")
            if 1 <= i < NS - 1:
                for t in range(LATE):
                    stage1_mm(*unit(i + 1), t)


QX = {1: [(1, 0), (1, 1)], 2: [(2, 0), (2, 1)], 3: [(3, 0)], 4: [(3, 1)]}
XE = {1: [(2, 0), (2, 1)], 2: [(3, 0), (3, 1)], 3: [(3, 2), (3, 3)]}
XL = {2: [(2, 2), (2, 3)]}
AFTER = (1,)
NB = 1
GO7 = (0,)
QB = 0
LATE = 3
GT8 = ()
TA, TB, QA = 1, 3, 1
EA = "S"
EC = "S"
GO = (0, 1)
CN = 3
